import numpy as np
CORES = [0,1,2,3,4,5,6,7]
N = 8
ROOT = 6
def setup_inputs(rng):
    return {"x": rng.standard_normal((N, 128, 4096), dtype=np.float32)}
def reference(x):
    return {"y": np.broadcast_to(x[ROOT], x.shape)}

@@ -1,0 +1,32 @@
+from concourse.bass import DstId, RemoteDMATransfer
+
+SCRATCH = {
+    "land": ("sbuf", [128, 4096], "float32"),
+}
+SEMAPHORES = ["loaded", "read", "arrived", "stored"]
+
+
+def rank_program(g, core, T, topo):
+    rank = T.rank_of(core)
+    if rank is None:
+        return
+    root = T.cores[6]
+    if core == root:
+        g.sync.dma_start(T.y[:], T.x[:]).then_inc(T.sem.stored, 16)
+        g.scalar.dma_start(T.land[:], T.x[:]).then_inc(T.sem.loaded, 16)
+        g.wait_ge(T.sem.loaded, 16)
+        others = [c for c in T.cores if c != root]
+        ids = []
+        for c in others:
+            rid, pid, _se = topo.addr(c)
+            ids.append(DstId(rid=rid, pnc=pid))
+        g.remote_dma_fused(
+            [RemoteDMATransfer(dst_ids=ids, dma_engine_mask=0xFFFF, remote_sem=T.sem.arrived,
+                               srcs=[T.land[:]], dsts=[T.land[:] for _c in others])],
+            local_sem=T.sem.read)
+        g.wait_ge(T.sem.read, 16)
+        g.wait_ge(T.sem.stored, 16)
+    else:
+        g.wait_ge(T.sem.arrived, 16)
+        g.dma_start(T.y[:], T.land[:]).then_inc(T.sem.stored, 16)
+        g.wait_ge(T.sem.stored, 16)

@@ -1,32 +1,71 @@
 from concourse.bass import DstId, RemoteDMATransfer
 
-SCRATCH = {
-    "land": ("sbuf", [128, 4096], "float32"),
-}
-SEMAPHORES = ["loaded", "read", "arrived", "stored"]
+ROOT_RANK = 6
+ROWS, COLS = 128, 4096
+N_RECV = 7
+N_PIECES = 2 * N_RECV
+ALL_ENGINES = 0xFFFF
+E = 16
+
+
+def _pieces():
+    base, extra = divmod(ROWS, N_PIECES)
+    out, r = [], 0
+    for j in range(N_PIECES):
+        n = base + (1 if j < extra else 0)
+        out.append((r, n))
+        r += n
+    return out
+
+
+PIECES = _pieces()
+
+SCRATCH = {"p%d" % j: ("dram", [128, n * COLS // 128], "float32") for j, (_r, n) in enumerate(PIECES)}
+SEMAPHORES = (["arr%d" % j for j in range(N_PIECES)] + ["ld%d" % j for j in range(N_PIECES)]
+              + ["sent", "stored", "go"])
 
 
 def rank_program(g, core, T, topo):
-    rank = T.rank_of(core)
-    if rank is None:
+    if T.rank_of(core) is None:
         return
-    root = T.cores[6]
+    root = T.cores[ROOT_RANK]
+    receivers = [c for c in T.cores if c != root]
+    local_queues = (g.sync, g.scalar)
+
     if core == root:
-        g.sync.dma_start(T.y[:], T.x[:]).then_inc(T.sem.stored, 16)
-        g.scalar.dma_start(T.land[:], T.x[:]).then_inc(T.sem.loaded, 16)
-        g.wait_ge(T.sem.loaded, 16)
-        others = [c for c in T.cores if c != root]
-        ids = []
-        for c in others:
-            rid, pid, _se = topo.addr(c)
-            ids.append(DstId(rid=rid, pnc=pid))
+        for j, (r, n) in enumerate(PIECES):
+            local_queues[j % 2].dma_start(T["p%d" % j][:], T.x[r:r + n, :]).then_inc(T.sem["ld%d" % j], E)
+        for j in range(N_PIECES):
+            rid, pid, _se = topo.addr(receivers[j % N_RECV])
+            g.wait_ge(T.sem["ld%d" % j], E)
+            g.remote_dma(T["p%d" % j][:], T["p%d" % j][:], T.sem["arr%d" % j], T.sem.sent, pid, rid, ALL_ENGINES)
+        g.sem_inc(T.sem.go, 1)
+        g.sync.wait_ge(T.sem.go, 1)
+        g.sync.dma_start(T.y[:], T.x[:]).then_inc(T.sem.stored, E)
+        g.wait_ge(T.sem.sent, E * N_PIECES)
+        g.wait_ge(T.sem.stored, E)
+        return
+
+    me = receivers.index(core)
+    peers = [c for c in receivers if c != core]
+    peer_ids = []
+    for c in peers:
+        rid, pid, _se = topo.addr(c)
+        peer_ids.append(DstId(rid=rid, pnc=pid))
+
+    mine = [j for j in range(N_PIECES) if j % N_RECV == me]
+    for j in mine:
+        p = T["p%d" % j]
+        g.wait_ge(T.sem["arr%d" % j], E)
         g.remote_dma_fused(
-            [RemoteDMATransfer(dst_ids=ids, dma_engine_mask=0xFFFF, remote_sem=T.sem.arrived,
-                               srcs=[T.land[:]], dsts=[T.land[:] for _c in others])],
-            local_sem=T.sem.read)
-        g.wait_ge(T.sem.read, 16)
-        g.wait_ge(T.sem.stored, 16)
-    else:
-        g.wait_ge(T.sem.arrived, 16)
-        g.dma_start(T.y[:], T.land[:]).then_inc(T.sem.stored, 16)
-        g.wait_ge(T.sem.stored, 16)
+            [RemoteDMATransfer(dst_ids=peer_ids, dma_engine_mask=ALL_ENGINES, remote_sem=T.sem["arr%d" % j],
+                               srcs=[p[:]], dsts=[p[:] for _c in peers])],
+            local_sem=T.sem.sent)
+
+    for j, (r, n) in enumerate(PIECES):
+        q = local_queues[j % 2]
+        q.wait_ge(T.sem["arr%d" % j], E)
+        q.dma_start(T.y[r:r + n, :], T["p%d" % j][:]).then_inc(T.sem.stored, E)
+
+    g.wait_ge(T.sem.sent, E * len(mine))
+    g.wait_ge(T.sem.stored, E * N_PIECES)

from concourse.bass import DstId, RemoteDMATransfer

ROOT_RANK = 6
ROWS, COLS = 128, 4096
N_RECV = 7
N_PIECES = 2 * N_RECV
ALL_ENGINES = 0xFFFF
E = 16


def _pieces():
    base, extra = divmod(ROWS, N_PIECES)
    out, r = [], 0
    for j in range(N_PIECES):
        n = base + (1 if j < extra else 0)
        out.append((r, n))
        r += n
    return out


PIECES = _pieces()

SCRATCH = {"p%d" % j: ("dram", [128, n * COLS // 128], "float32") for j, (_r, n) in enumerate(PIECES)}
SEMAPHORES = (["arr%d" % j for j in range(N_PIECES)] + ["ld%d" % j for j in range(N_PIECES)]
              + ["sent", "stored", "go"])


def rank_program(g, core, T, topo):
    if T.rank_of(core) is None:
        return
    root = T.cores[ROOT_RANK]
    receivers = [c for c in T.cores if c != root]
    local_queues = (g.sync, g.scalar)

    if core == root:
        for j, (r, n) in enumerate(PIECES):
            local_queues[j % 2].dma_start(T["p%d" % j][:], T.x[r:r + n, :]).then_inc(T.sem["ld%d" % j], E)
        for j in range(N_PIECES):
            rid, pid, _se = topo.addr(receivers[j % N_RECV])
            g.wait_ge(T.sem["ld%d" % j], E)
            g.remote_dma(T["p%d" % j][:], T["p%d" % j][:], T.sem["arr%d" % j], T.sem.sent, pid, rid, ALL_ENGINES)
        g.sem_inc(T.sem.go, 1)
        g.sync.wait_ge(T.sem.go, 1)
        g.sync.dma_start(T.y[:], T.x[:]).then_inc(T.sem.stored, E)
        g.wait_ge(T.sem.sent, E * N_PIECES)
        g.wait_ge(T.sem.stored, E)
        return

    me = receivers.index(core)
    peers = [c for c in receivers if c != core]
    peer_ids = []
    for c in peers:
        rid, pid, _se = topo.addr(c)
        peer_ids.append(DstId(rid=rid, pnc=pid))

    mine = [j for j in range(N_PIECES) if j % N_RECV == me]
    for j in mine:
        p = T["p%d" % j]
        g.wait_ge(T.sem["arr%d" % j], E)
        g.remote_dma_fused(
            [RemoteDMATransfer(dst_ids=peer_ids, dma_engine_mask=ALL_ENGINES, remote_sem=T.sem["arr%d" % j],
                               srcs=[p[:]], dsts=[p[:] for _c in peers])],
            local_sem=T.sem.sent)

    for j, (r, n) in enumerate(PIECES):
        q = local_queues[j % 2]
        q.wait_ge(T.sem["arr%d" % j], E)
        q.dma_start(T.y[r:r + n, :], T["p%d" % j][:]).then_inc(T.sem.stored, E)

    g.wait_ge(T.sem.sent, E * len(mine))
    g.wait_ge(T.sem.stored, E * N_PIECES)
